import numpy as np, ml_dtypes
CORES = [33,161,289,417,57,185,313,441]
N = 8
R, L = 4096, 1024
CAPP = 256
def entries(a): return a.T.reshape(-1)
def pack(v, P): return np.ascontiguousarray(np.asarray(v, np.int32).reshape(-1, P).T)
def lists(rng, how):
    n = N * L; own = np.arange(n) // L
    P = rng.permutation(np.repeat(np.arange(N * N), CAPP))
    if how == "neg": P = rng.permutation(P[np.argsort(P // N != P % N, kind="stable")][:n])
    P = P[:n]
    if how == "full":
        a = rng.integers(0, N); o = rng.permutation(N * N); o = o[(o // N != a) & (o % N != a)]; e = np.delete(np.arange(N), a)
        C = np.concatenate([N * a + rng.permutation(e), [N * a + a], N * rng.permutation(e) + a, o])[:n // CAPP]
        P = np.repeat(C, CAPP).reshape(N, L)[rng.permutation(N)]; P[1::2] = rng.permuted(P[1::2], axis=1); P = P.reshape(-1)
    h, g = P // N, P % N
    if how == "meet":
        z = rng.permutation(N)[:3]; p = CAPP // N; e = np.delete(np.arange(N), z[1:])
        g = np.tile(np.concatenate([np.repeat(z[1:], p), np.repeat(z[1:], CAPP % N), e, rng.permutation(np.repeat(e, CAPP - 1))[:L - 2 * (p + CAPP % N) - len(e)]]), N)
        h = (own + np.tile(rng.integers(0, N, L), N)) % N; h.reshape(N, L)[:, :2 * p] = np.repeat(z[[0, 2]], p)
    d = np.zeros(n, np.int64)
    for q in range(N):
        for r in range(N):
            if r == 0 or how != "meet": c = R * q + np.concatenate([[0, R - 1], 1 + rng.permutation(R - 2)])
            m = L * r + np.nonzero(g[L * r:L * r + L] == q)[0]; d[m] = c[:len(m)]
    s = R * h + rng.integers(0, R, n)
    if how == "fork": s = R * h + rng.integers(0, R, N)[h]
    if how == "meet":
        for q in range(N): m = np.nonzero(h == q)[0]; w = d[:L][g[:L] == q]; s[m] = w[rng.integers(0, len(w), len(m))]
        s.reshape(N, L)[:, :2 * p] = R * h.reshape(N, L)[:, :2 * p] + rng.permutation(R)[:2 * p * N].reshape(N, 2 * p)
        o = (L * np.arange(N)[:, None] + rng.permuted(np.tile(np.arange(L), (N, 1)), axis=1)).reshape(-1); s, d = s[o], d[o]
    if how == "neg": s = np.where(h == g, d, s)
    if how == "gaps":
        z = rng.permutation(N)[:3]; k = (rng.random(n) < 0.5) | (own == z[0]) | (h == z[1]) | (g == z[2]); s[k] = -1; d[k] = -1
    out = {"src": np.stack([pack(v, 16) for v in s.reshape(N, L)]), "dst": np.stack([pack(v, 16) for v in d.reshape(N, L)])}
    if how == "neg": out["tab"] = (-(0.5 + np.minimum(np.abs(rng.standard_normal((N, 128, R), dtype=np.float32)), 7)) * (2.0 ** rng.permuted(np.tile(np.arange(R) % 97, (N, 1)), axis=1)).astype(np.float32)[:, None, :]).astype(ml_dtypes.bfloat16)
    return out
def setup_inputs(rng):
    return dict({"tab": rng.standard_normal((N, 128, R), dtype=np.float32).astype(ml_dtypes.bfloat16)}, **lists(rng, "uniform"))
def setup_inputs_fork(rng):
    d = setup_inputs(rng); d.update(lists(rng, "fork"))
    for k in ("tab",): d[k] = (d[k].astype(np.float32) * 1048576.0).astype(d[k].dtype)
    return d
def setup_inputs_full(rng):
    d = setup_inputs(rng); d.update(lists(rng, "full"))
    for k in ("tab",): d[k] = (d[k].astype(np.float32) * (1 / 1024.0)).astype(d[k].dtype)
    return d
def setup_inputs_gaps(rng):
    d = setup_inputs(rng); d.update(lists(rng, "gaps"))
    return d
def setup_inputs_meet(rng):
    d = setup_inputs(rng); d.update(lists(rng, "meet"))
    return d
def setup_inputs_neg(rng):
    d = setup_inputs(rng); d.update(lists(rng, "neg"))
    return d
def check_inputs(x):
    bad = []; S, D = x["src"].reshape(-1), x["dst"].reshape(-1); K = (S >= 0) & (D >= 0)
    if S.min() < -1 or S.max() >= N * R or D.min() < -1 or D.max() >= N * R: bad.append("out of range")
    if ((S < 0) != (D < 0)).any(): bad.append("half an edge")
    for a in x["dst"]:
        if len(np.unique(a[a >= 0])) != int((a >= 0).sum()): bad.append("a column is named by two dst of one list")
    if K.any() and int(np.bincount(S[K] // R * N + D[K] // R).max()) > CAPP: bad.append("more than CAPP edges from one rank's part to one rank's part")
    if np.abs(x["tab"].astype(np.float32)).max() > 1e30: bad.append("tab beyond -1e30 to 1e30")
    return bad
def reference(tab, src, dst):
    A = np.concatenate(list(tab), axis=1); Y = A.copy()
    for r in range(N):
        s, d = entries(src[r]), entries(dst[r]); k = d >= 0
        Y[:, d[k]] = np.maximum(Y[:, d[k]], A[:, s[k]])
    return {"y": np.stack([Y[:, R * r:R * r + R] for r in range(N)])}

from concourse.bass import DstId, RemoteDMATransfer
from concourse.mybir import AluOpType as A, ActivationFunctionType as AF

NR, CAP = 8, 256
WIN = 4096 + 1152
SCRATCH = {
    "big": ("dram", [8, 128, 16], "int32"),
    "ps": ("psum", [128, 4096], "float32"),
    "tabs": ("sbuf", [128, WIN], "bfloat16"),
    "w2": ("sbuf", [128, WIN], "bfloat16"),
    "land": ("sbuf", [128, 2048], "bfloat16"),
    "snd": ("sbuf", [128, 1024], "bfloat16"),
    "rel": ("sbuf", [128, 512], "bfloat16"),
    "idx": ("sbuf", [128, 512], "uint16"),
    "fl": ("sbuf", [128, 16 + 2048], "bfloat16"),
    "xx": ("sbuf", [128, 2048], "bfloat16"),
    "yb": ("sbuf", [128, 4096], "bfloat16"),
    "so": ("sbuf", [128, 2064], "bfloat16"),
    "dm": ("sbuf", [128, 2048], "bfloat16"),
    "it3": ("sbuf", [128, 128], "int32"), "it4": ("sbuf", [128, 16], "int32"),
    "lc": ("sbuf", [128, 128], "float32"), "col": ("sbuf", [128, 16], "float32"),
    "gg": ("sbuf", [128, 264], "float32"), "gh": ("sbuf", [128, 136], "float32"), "rst": ("sbuf", [128, 264], "float32"),
    "ind": ("sbuf", [128, 528], "bfloat16"), "hl": ("sbuf", [128, 128], "bfloat16"), "dlb": ("sbuf", [128, 64], "bfloat16"),
    "flat": ("sbuf", [128, 1024], "bfloat16"), "tv": ("sbuf", [128, 16], "bfloat16"),
}
for _n in ("S", "D", "itt", "t1", "t2", "t3", "key", "sl", "u", "dlo", "ddh", "dof"):
    SCRATCH[_n] = ("sbuf", [128, 64], "int32")
for _n in ("it1", "it2", "ci", "cj"):
    SCRATCH[_n] = ("sbuf", [128, 128], "int32")
for _n in ("tri", "one", "e16", "la"):
    SCRATCH[_n] = ("sbuf", [128, 128], "bfloat16")
for _n in ("za", "zb", "bd"):
    SCRATCH[_n] = ("sbuf", [128, 160], "bfloat16")
for _n in ("sc", "ff"):
    SCRATCH[_n] = ("sbuf", [128, 528], "float32")
for _n in ("zer", "sb", "q1", "q2", "q3", "q4"):
    SCRATCH[_n] = ("sbuf", [128, 256], "float32")
for _n in ("fu", "g2", "g3"):
    SCRATCH[_n] = ("sbuf", [128, 64], "float32")
for _n in ("off", "goff", "offd", "ddo"):
    SCRATCH[_n] = ("sbuf", [128, 64], "uint16")
SEMAPHORES = ["sv", "ss", "sp", "sg", "ld", "lo", "lc2", "lx", "sd", "tl", "tq", "da", "r0", "r1", "iv", "ih", "d1", "yd", "lsem"]


def neighbours(T, topo, r):
    c = T.cores[r]
    rk = cb = xx = None
    for q in range(NR):
        d = T.cores[q]
        if q == r:
            continue
        if topo.host(d) == topo.host(c):
            xx = q
        elif topo.chip(d) == topo.chip(c):
            if topo.rack(topo.host(d)) == topo.rack(topo.host(c)):
                rk = q
            elif topo.may_write(c, d):
                cb = q
    return rk, cb, xx


def crew(T, topo, r):
    p = T.cores[r]
    other = T.cores[neighbours(T, topo, r)[2]]
    per = topo.CORES_PER_HOST
    sib = [c for c in range(topo.host(p) * per, (topo.host(p) + 1) * per) if topo.chip(c) == topo.chip(p) and c != p]
    q = [c for c in sib if topo.die(c) != topo.die(p) and topo.may_write(c, other)][0]
    rr = [c for c in sib if topo.die(c) == topo.die(p)][-1]
    return p, q, rr


def bits(mask):
    return [1 << i for i in range(16) if (mask >> i) & 1]


def rank_program(g, core, T, topo):
    me = None
    for r in range(NR):
        c = T.cores[r]
        if topo.host(c) == topo.host(core) and topo.chip(c) == topo.chip(core):
            me = r
    if me is None:
        return
    crews = [crew(T, topo, r) for r in range(NR)]
    if core not in crews[me]:
        return
    role = crews[me].index(core)
    nb = [neighbours(T, topo, r) for r in range(NR)]
    rack, cab, xh = nb[me]
    V, SC, PE = g.vector, g.scalar, g.tensor
    queue = {"v": V, "s": SC, "p": PE, "g": g, "y": g.sync}
    own = {"v": "sv", "s": "ss", "p": "sp", "g": "sg"}
    cnt = {"v": 0, "s": 0, "p": 0, "g": 0}
    seen = {}

    def wait(q, name, val):
        if seen.get((q, name), 0) < val:
            queue[q].wait_ge(T.sem[name], val)
            seen[(q, name)] = val

    def op(q, deps, fn, *a, **k):
        need = {}
        for d in deps:
            if d is not None:
                need[d[0]] = max(need.get(d[0], 0), d[1])
        for nm in need:
            wait(q, nm, need[nm])
        fn(*a, **k).then_inc(T.sem[own[q]], 1)
        cnt[q] += 1
        return (own[q], cnt[q])

    def ts(deps, out, in0, s1, s2, o0, o1=None):
        if o1 is None:
            return op("v", deps, V.tensor_scalar, out, in0, s1, None, o0)
        return op("v", deps, V.tensor_scalar, out, in0, s1, s2, o0, o1)

    def tt(deps, out, a, b, o):
        return op("v", deps, V.tensor_tensor, out, a, b, o)

    def cp(deps, out, a):
        return op("v", deps, V.tensor_copy, out, a)

    def ms(ap, c, deps=()):
        return op("v", deps, V.memset, ap, c)

    def mm(deps, out, l, r, st=True, sp=True):
        return op("p", deps, PE.matmul, out, l, r, st, sp)

    def bank(i, a, b):
        return T.ps[:, 512 * i + a:512 * i + b]

    sent = [0]

    def send(dst, out, src, sem, mask):
        rid, pid = topo.addr(dst, core)
        g.remote_dma(out, src, T.sem[sem], T.sem.lsem, pid, rid, mask)
        sent[0] += len(bits(mask))

    def move(dsts, slot, sem, mask):
        ids = []
        for d in dsts:
            rid, pid = topo.addr(d, core)
            ids.append(DstId(rid=rid, pnc=pid))
        sent[0] += len(bits(mask))
        return RemoteDMATransfer(dst_ids=ids, dma_engine_mask=mask, remote_sem=T.sem[sem], srcs=[T.big[slot]], dsts=[T.big[slot]] * len(dsts))

    offm = topo.mask(core, T.cores[rack])
    onm = topo.mask(core, [c for c in crews[me] if c != core][0])
    ob = bits(offm)
    four = ob[0] | ob[2] | ob[4] | ob[6]
    half = bits(onm & ~offm)

    if role == 0:
        g.sync.dma_start(T.big[me, 0:64, :], T.src[:, :]).then_inc(T.sem.ld, 16)
        SC.dma_start(T.big[me, 64:128, :], T.dst[:, :]).then_inc(T.sem.ld, 16)
        g.sync.dma_start(T.tabs[:, 0:2048], T.tab[:, 0:2048]).then_inc(T.sem.tl, 16)
        SC.dma_start(T.tabs[:, 2048:4096], T.tab[:, 2048:4096]).then_inc(T.sem.tl, 16)

    tA = op("g", [], g.iota, T.it1[:, :], [[-1, 16], [-16, 8]], 0, 1)
    tB = op("g", [], g.iota, T.it2[:, :], [[1, 128]], 0, -1)
    tbase = 1024 if role < 2 else 4096
    tT = op("g", [], g.iota, T.itt[:, :], [[16, 64]], tbase, 1)
    if role == 2:
        tC = op("g", [], g.iota, T.it3[:, :], [[0, 8], [1, 16]], 0, -1)
        tD = op("g", [], g.iota, T.it4[:, 0:8], [[-16, 8]], 0, 1)
        tE = op("g", [], g.iota, T.it4[:, 8:9], [[0, 1]], 0, 1)

    if role == 0:
        wait("g", "ld", 32)
        g.remote_dma_fused([
            move(crews[rack], me, "lx", ob[0] | ob[2]),
            move(crews[cab], me, "lc2", ob[4] | ob[6]),
            move(crews[me][1:], me, "lo", half[0] | half[2]),
        ], local_sem=T.sem.lsem)
        wait("g", "tl", 32)
        send(crews[me][1], T.tabs[:, 0:4096], T.tabs[:, 0:4096], "tq", onm)
    elif role == 1:
        tgt = list(crews[xh]) + list(crews[nb[xh][0]])
        wait("g", "lo", 2)
        g.remote_dma_fused([move(tgt, me, "lx", four)], local_sem=T.sem.lsem)
        wait("g", "lc2", 2)
        g.remote_dma_fused([move(tgt, cab, "lx", four)], local_sem=T.sem.lsem)
    else:
        wait("g", "lc2", 2)
        g.remote_dma_fused([move(crews[rack], cab, "lx", four)], local_sem=T.sem.lsem)
    lists = [("lc2", 2), ("lx", 22)] + ([("ld", 32)] if role == 0 else [("lo", 2)])
    for q, buf, a in (("y", T.S, 0), ("s", T.D, 64)):
        for nm, val in lists:
            wait(q, nm, val)
        queue[q].dma_start(buf[:, :], T.big[:, a:a + 64, :]).then_inc(T.sem.sd, 16)
    tS = ("sd", 32)

    ncl = 4 if role < 2 else 8
    k1 = ms(T.fl[:, :], 0.0)
    ts([tA, k1], T.fl[:, 16:2064:16], T.it1[:, :], 0, None, A.is_equal)
    kTri = ts([tB], T.tri[:, :], T.it2[:, :], 0, None, A.is_gt)
    kOne = ms(T.one[:, :], 1.0)
    k1 = ms(T.za[:, :], 0.0)
    ms(T.rst[:, :], 1.0)
    k2 = ms(T.ind[:, :], 0.0)
    for b in range(ncl):
        ms(T.ind[:, 65 * b:65 * b + 1], float(2 * b), [k2])
    for b in range(4):
        ms(T.rst[:, 65 * b:65 * b + 1], 0.0, [k2])
    if role < 2:
        ms(T.za[:, 0:160:16], 1.0, [k1])
        ms(T.w2[:, 0:1024], 0.0)
    else:
        ms(T.tabs[:, 0:4096], 0.0)
        ms(T.w2[:, 0:4096], 0.0)
        ms(T.snd[:, :], 1.0)
        ms(T.zer[:, :], 0.0)
        k3 = ms(T.zb[:, :], 0.0)
        k4 = ms(T.bd[:, :], 0.0)
        k5 = ts([tB, kTri], T.cj[:, :], T.it2[:, :], 15, None, A.bitwise_and)
        kE16 = ts([k5], T.e16[:, :], T.cj[:, :], 0, None, A.is_equal)
        tt([kE16, kTri], T.la[:, :], T.e16[:, :], T.tri[:, :], A.mult)
        ts([tC], T.lc[:, :], T.it3[:, :], 0, None, A.is_gt)
        k6 = ts([tD], T.ci[:, 0:8], T.it4[:, 0:8], 4, None, A.arith_shift_right)
        ts([k6, k4], T.bd[:, 16:144:16], T.ci[:, 0:8], 0, None, A.is_equal)
        k7 = ts([tE], T.it4[:, 9:10], T.it4[:, 8:9], 15, None, A.bitwise_and)
        cp([k7], T.col[:, 0:1], T.it4[:, 9:10])
        kP2 = ts([k7], T.col[:, 1:2], T.it4[:, 9:10], 2, None, A.is_equal)
        k8 = ts([k7], T.col[:, 2:3], T.it4[:, 9:10], 1, None, A.is_le)
        k9 = ts([kP2], T.col[:, 3:4], T.col[:, 1:2], 4096, None, A.mult)
        k9 = tt([k8, k9], T.col[:, 4:5], T.col[:, 2:3], T.col[:, 3:4], A.add)
        ts([k8, k3, kOne], T.zb[:, 0:160:16], T.one[:, 0:10], T.col[:, 2:3], None, A.mult)
        ts([k9, k1, kOne], T.za[:, 0:160:16], T.one[:, 0:10], T.col[:, 4:5], None, A.mult)
        for i in range(16):
            ts([tA], T.xx[:, i:2048:16], T.it1[:, :], 0, None, A.is_equal)
    if role == 0:
        ms(T.tv[:, 0:1], 9e29)
        k1 = ms(T.tv[:, 1:2], -9e29)
        kTv = ts([k1], T.tv[:, 0:2], T.tv[:, 0:2], 64.0, None, A.mult)
        cp([kTv], T.so[:, 2048:2049], T.tv[:, 1:2])
    kAll = ("sv", cnt["v"])

    def flatten(h, deps):
        t = None
        for i in range(8 * h, 8 * h + 8):
            o = bank(h, 64 * (i - 8 * h), 64 * (i - 8 * h) + 64)
            t = mm(deps, o, T.fl[:, 16 + 128 * i:144 + 128 * i], T.hl[:, 0:64], True, False)
            t = mm(deps, o, T.fl[:, 15 + 128 * i:143 + 128 * i], T.hl[:, 64:128], False, True)
        return t

    def unroll(h, dst, at, dep, bias=None):
        t = None
        for i in range(8 * h, 8 * h + 8):
            o, s = dst[:, at + i:at + 1024:16], bank(h, 64 * (i - 8 * h), 64 * (i - 8 * h) + 64)
            if bias is None:
                t = op("s", dep, SC.activation, o, s, AF.Copy)
            else:
                t = op("s", dep, SC.activation, o, s, AF.Identity, bias=bias)
        return t

    def prefix(h, tI):
        a = mm([tI, kAll], bank(4 + h, 0, 260), T.one[:, :], T.ind[:, 260 * h:260 * h + 260])
        b = mm([tI, kAll], bank(2 + h, 0, 260), T.tri[:, :], T.ind[:, 260 * h:260 * h + 260])
        return a, b

    def slots(h, x, out):
        o = 260 * h
        s = op("v", [x[0]], V.tensor_tensor_scan, T.sc[:, o:o + 260], T.rst[:, 0:260], bank(4 + h, 0, 260), 0.0, A.mult, A.add)
        e = tt([s, x[1]], bank(2 + h, 1, 260), T.sc[:, o:o + 259], bank(2 + h, 1, 260), A.add)
        return tt([e], out, bank(2 + h, 1, 260), T.ind[:, o + 1:o + 260], A.mult)

    def fold4(src, dep):
        a = tt([dep], T.gh[:, 0:129], src[:, 0:129], src[:, 130:259], A.add)
        return tt([a], T.g2[:, :], T.gh[:, 0:64], T.gh[:, 65:129], A.add)

    if role < 2:
        ref = me if role == 0 else xh
        b0 = 4 * (ref // 4)
        s1 = ts([tS], T.sl[:, :], T.S[:, :], 4095, None, A.bitwise_and)
        a1 = ts([tS], T.t1[:, :], T.S[:, :], 12, None, A.arith_shift_right)
        a2 = ts([tS], T.t2[:, :], T.D[:, :], 12, None, A.arith_shift_right)
        s2 = cp([s1], T.hl[:, 0:64], T.sl[:, :])
        a3 = ts([a1], T.t3[:, :], T.t1[:, :], me, 64, A.not_equal, A.mult)
        s3 = tt([s2], T.hl[:, 64:128], T.sl[:, :], T.hl[:, 0:64], A.subtract)
        f0 = flatten(0, [s3, kAll])
        a4 = tt([a3, a2], T.key[:, :], T.t3[:, :], T.t2[:, :], A.add)
        for b in range(4):
            tI = ts([a4], T.ind[:, 65 * b + 1:65 * b + 65], T.key[:, :], b0 + b, None, A.is_equal)
        x = prefix(0, tI)
        f1 = flatten(1, [s3])
        unroll(0, T.flat, 0, [f0])
        c1 = unroll(1, T.flat, 0, [f1])
        u = ts([a4], T.t1[:, :], T.key[:, :], 2, None, A.arith_shift_right)
        u = ts([u], T.u[:, :], T.t1[:, :], b0 // 4, None, A.not_equal)
        u = tt([u, tT], T.fu[:, :], T.u[:, :], T.itt[:, :], A.mult)
        s = slots(0, x, T.ff[:, 0:259])
        s = fold4(T.ff, s)
        s = tt([s, u], T.g3[:, :], T.g2[:, :], T.fu[:, :], A.add)
        s = cp([s], T.off[:, :], T.g3[:, :])
        s = cp([s, c1], T.w2[:, 0:2176].indirect(T.off[:, 0:64]), T.flat[:, :])
        for i in range(16):
            m = mm([s], bank(6, 0, 64), T.za[:, 16 - i:144 - i], T.w2[:, i:1024:16], i == 0, i == 15)
        go = cp([m], T.goff[:, :], bank(6, 0, 64))
        ttab = ("tl", 32) if role == 0 else ("tq", 16)
        rk2, cb2 = nb[ref][0], nb[ref][1]
        dg2 = nb[rk2][1]
        tok = {}
        for n, b in enumerate((dg2, cb2, rk2, ref)):
            j = b - b0
            out = T.snd[:, 256 * j:256 * j + 256] if b != me else T.land[:, 256 * me:256 * me + 256]
            src = T.tabs[:, 0:4096].indirect(T.goff[:, 16 * j:16 * j + 16])
            if n % 2 == 0:
                tok[b] = op("v", [go, ttab], V.tensor_copy, out, src)
            else:
                tok[b] = op("s", [go, ttab], SC.activation, out, src, AF.Copy)
        for b in (dg2, cb2, rk2, ref):
            if b == me:
                continue
            wait("g", *tok[b])
            src = T.snd[:, 256 * (b - b0):256 * (b - b0) + 256]
            if b == dg2:
                send(crews[rk2][2], T.rel[:, 256 * role:256 * role + 256], src, "r%d" % role, offm)
            else:
                send(T.cores[b], T.land[:, 256 * me:256 * me + 256], src, "da", offm)

    if role == 2:
        a1 = ts([tS], T.t2[:, :], T.D[:, :], 12, None, A.arith_shift_right)
        a2 = ts([tS], T.dlo[:, :], T.D[:, :], 15, None, A.bitwise_and)
        a3 = ts([tS], T.ddh[:, :], T.D[:, :], 4095, 4, A.bitwise_and, A.arith_shift_right)
        a4 = ts([a1], T.u[:, :], T.t2[:, :], me, None, A.not_equal)
        a5 = ts([a2], T.sl[:, :], T.dlo[:, :], 256, None, A.mult)
        a6 = ts([a4], T.t3[:, :], T.u[:, :], 64, None, A.mult)
        fu = tt([a4, tT], T.fu[:, :], T.u[:, :], T.itt[:, :], A.mult)
        a7 = tt([a5, a3], T.dof[:, :], T.sl[:, :], T.ddh[:, :], A.add)
        db = tt([a6], T.dlb[:, :], T.dlo[:, :], T.t3[:, :], A.add)
        a8 = tt([a7, fu], T.g3[:, :], T.dof[:, :], T.fu[:, :], A.max)
        for h in range(2):
            for i in range(8 * h, 8 * h + 8):
                m = mm([db, kAll], bank(h, 64 * (i - 8 * h), 64 * (i - 8 * h) + 64), T.xx[:, 128 * i:128 * i + 128], T.dlb[:, :])
            dc = unroll(h, T.yb, 3072, [m])
        a9 = cp([a8], T.offd[:, :], T.g3[:, :])
        w1 = cp([a9], T.tabs[:, 0:WIN].indirect(T.offd[:, 0:64]), T.snd[:, :])
        wait("y", *w1)
        g.sync.dma_start(T.dm[:, 0:256], T.tabs[0:128:16, 0:4096]).then_inc(T.sem.d1, 16)
        b1 = ts([], T.t1[:, :], T.S[:, :], 12, None, A.arith_shift_right)
        b2 = tt([b1, a6], T.key[:, :], T.t1[:, :], T.t3[:, :], A.add)
        dd = cp([], T.ddo[:, :], T.ddh[:, :])
        for a in range(8):
            tI = ts([b2], T.ind[:, 65 * a + 1:65 * a + 65], T.key[:, :], a, None, A.is_equal)
            if a == 3:
                x0 = prefix(0, tI)
        x1 = prefix(1, tI)
        mk = ts([dc], T.yb[:, 2048:3072], T.yb[:, 3072:4096], T.col[:, 0:1], None, A.is_equal)
        f0 = slots(0, x0, T.ff[:, 0:259])
        f1 = slots(1, x1, bank(3, 1, 260))
        f = tt([f0, f1], T.gg[:, 0:259], T.ff[:, 0:259], bank(3, 1, 260), A.add)
        f = fold4(T.gg, f)
        h1 = cp([f], T.hl[:, 0:64], T.g2[:, :])
        h2 = tt([h1], T.hl[:, 64:128], T.g2[:, :], T.hl[:, 0:64], A.subtract)
        mB = mm([("d1", 16)], bank(7, 0, 256), T.e16[:, :], T.dm[:, 0:256])
        mA = mm([], bank(6, 0, 256), T.la[:, :], T.dm[:, 0:256])
        q = op("v", [mB], V.tensor_tensor_scan, T.sb[:, :], bank(7, 0, 256), T.zer[:, :], 0.0, A.add, A.add)
        mC = mm([q], bank(4, 0, 1), T.lc[:, :], T.sb[:, 255:256])
        fa = flatten(0, [h2, dc])
        unroll(0, T.flat, 0, [fa], T.col[:, 1:2])
        q1 = tt([q], T.q1[:, :], T.sb[:, :], bank(7, 0, 256), A.subtract)
        q2 = ts([mA], T.q2[:, :], bank(6, 0, 256), 0, 2048, A.is_equal, A.mult)
        q3 = tt([q1], T.q3[:, :], T.q1[:, :], bank(6, 0, 256), A.add)
        q4 = tt([q3, q2], T.q4[:, :], T.q3[:, :], T.q2[:, :], A.add)
        gh = ts([q4, mC], T.so[:, 0:256], T.q4[:, :], bank(4, 0, 1), None, A.add)
        g3 = ts([q4, mC], T.q3[:, :], T.q4[:, :], bank(4, 0, 1), None, A.add)
        zh = tt([gh, mk, dd], T.yb[:, 0:1024], T.so[:, 0:256].indirect(T.ddo[:, 0:64]), T.yb[:, 2048:3072], A.mult)
        gl = tt([g3, gh], T.so[:, 256:512], T.q3[:, :], T.so[:, 0:256], A.subtract)
        zl = tt([gl], T.yb[:, 1024:2048], T.so[:, 256:512].indirect(T.ddo[:, 0:64]), T.yb[:, 2048:3072], A.mult)
        fb = flatten(1, [h2, dc])
        c1 = unroll(1, T.flat, 0, [fb], T.col[:, 1:2])
        for i in range(16):
            m = mm([zh], bank(5, 0, 64), T.bd[:, 16 - i:144 - i], T.yb[:, i:1024:16], i == 0, False)
        for i in range(16):
            m = mm([zl], bank(5, 0, 64), T.bd[:, 16 - i:144 - i], T.yb[:, 1024 + i:2048:16], False, i == 15)
        o = tt([m], T.g3[:, :], bank(5, 0, 64), T.fu[:, :], A.max)
        o = cp([o], T.off[:, :], T.g3[:, :])
        w = cp([o, c1], T.w2[:, 0:WIN].indirect(T.off[:, 0:64]), T.flat[:, :])
        for k, z in enumerate((T.zb, T.za)):
            for i in range(16):
                m = mm([w], bank(2, 0, 128), z[:, 16 - i:144 - i], T.w2[:, 2048 * k + i:2048 * k + 2048:16], k == 0 and i == 0, k == 1 and i == 15)
        e1 = ts([], T.q1[:, :], T.sb[:, :], bank(4, 0, 1), -2049, A.add, A.add)
        e2 = ts([], T.q2[:, :], bank(7, 0, 256), 0, None, A.is_gt)
        e3 = tt([e1, e2], T.q4[:, :], T.q1[:, :], T.q2[:, :], A.mult)
        e4 = ts([e3], T.idx[:, 256:512], T.q4[:, :], 2048, None, A.add)
        d1 = cp([m], T.ci[:, :], bank(2, 0, 128))
        d2 = ts([m], T.idx[:, 128:256], bank(2, 0, 128), 4096, None, A.is_ge)
        d3 = ts([d1], T.cj[:, :], T.ci[:, :], 4095, None, A.bitwise_and)
        d4 = cp([d3], T.idx[:, 0:128], T.cj[:, :])
        pc = T.cores[me]
        for k, a in ((0, rack), (1, nb[rack][2])):
            wait("g", "r%d" % k, 8)
            send(T.cores[cab], T.land[:, 256 * a:256 * a + 256], T.rel[:, 256 * k:256 * k + 256], "da", offm)
        wait("g", *e4)
        send(pc, T.idx[:, 256:512], T.idx[:, 256:512], "iv", offm)
        wait("g", *d2)
        wait("g", *d4)
        send(pc, T.idx[:, 0:256], T.idx[:, 0:256], "ih", offm)

    if role == 0:
        ih, iv, da = ("ih", 8), ("iv", 8), ("da", 56)
        m0 = op("v", [ih, kAll], V.tensor_copy, T.dm[:, 0:1024], T.tv[:, 0:2].indirect(T.idx[:, 128:192]))
        m1 = op("s", [ih, kAll], SC.activation, T.dm[:, 1024:2048], T.tv[:, 0:2].indirect(T.idx[:, 192:256]), AF.Copy)
        x0 = op("v", [da, tok[me]], V.tensor_copy, T.xx[:, 0:1024], T.land[:, :].indirect(T.idx[:, 0:64]))
        x1 = op("s", [da, tok[me]], SC.activation, T.xx[:, 1024:2048], T.land[:, :].indirect(T.idx[:, 64:128]), AF.Copy)
        s0 = op("v", [x0, m0], V.tensor_tensor_scan, T.so[:, 0:1024], T.dm[:, 0:1024], T.xx[:, 0:1024], 0.0, A.min, A.max)
        s1 = op("v", [s0, x1, m1], V.tensor_tensor_scan, T.so[:, 1024:2048], T.dm[:, 1024:2048], T.xx[:, 1024:2048], T.so[:, 1023:1024], A.min, A.max)
        for k in range(4):
            c = slice(1024 * k, 1024 * k + 1024)
            y = tt([s1, iv], T.yb[:, c], T.so[:, 0:2049].indirect(T.idx[:, 256 + 64 * k:320 + 64 * k]), T.tabs[:, c], A.max)
            q = "y" if k % 2 == 0 else "s"
            wait(q, *y)
            queue[q].dma_start(T.y[:, c], T.yb[:, c]).then_inc(T.sem.yd, 16)
        wait("g", "yd", 64)

    for q in ("v", "s", "p", "g"):
        if cnt[q]:
            wait("g", own[q], cnt[q])
    for nm, val in lists + [tS]:
        wait("g", nm, val)
    wait("g", "lsem", sent[0])
    if role == 0:
        for nm, val in (("tl", 32), ("da", 56), ("ih", 8), ("iv", 8)):
            wait("g", nm, val)
    if role == 1:
        wait("g", "tq", 16)
    if role == 2:
        wait("g", "d1", 16)
